import numpy as np
import ml_dtypes


def mxq(x, axis, fmt="e4m3"):
    dtype, down = {"e4m3": (ml_dtypes.float8_e4m3fn, 7), "e5m2": (ml_dtypes.float8_e5m2, 14)}[fmt]
    v = np.moveaxis(np.asarray(x, np.float32).astype(ml_dtypes.bfloat16).astype(np.float64), axis, -1)
    blocks = v.reshape(v.shape[:-1] + (-1, 32))
    amax = np.abs(blocks).max(-1, keepdims=True)
    byte = np.maximum(np.where(amax > 0, np.frexp(amax)[1] - 1 + 127, 0) - down, 1)
    scale = np.exp2(byte - 127.0)
    codes = (blocks / scale).astype(np.float32).astype(dtype).astype(np.float64)
    return np.moveaxis((codes * scale).reshape(v.shape), -1, axis)


WIDE = False


def mx_kscale(k):
    if not WIDE:
        return np.ones(k)
    levels = np.array([30, -30])
    if k % 512:
        return np.exp2(np.random.permutation(np.resize(levels, k // 32))).repeat(32)
    a = np.empty((k // 512, 16))
    for p in range(k // 512):
        a[p, :8] = np.random.permutation(np.resize(levels, 8))
        for g in range(8):
            far = levels[np.abs(levels - a[p, g]) >= 10]
            a[p, g + 8] = far[np.random.randint(len(far))]
    return np.exp2(a.ravel()).repeat(32)


def f64(x):
    return np.asarray(x).astype(np.float64)


def striped(idx):
    return np.tile(np.asarray(idx).reshape(-1, 16).T, (8, 1)).astype(np.uint16)


def unstriped(offs):
    return offs[:16].T.reshape(-1).astype(np.int64)


E2M1 = np.array([0.0, 0.5, 1.0, 1.5, 2.0, 3.0, 4.0, 6.0, -0.0, -0.5, -1.0, -1.5, -2.0, -3.0, -4.0, -6.0])


def pack_weight(w, fmt):
    k, n = w.shape
    w = f64(np.asarray(w, np.float32).astype(ml_dtypes.bfloat16)).reshape(k // 32, 32, n)
    amax = np.abs(w).max(1)
    if fmt in ("e4m3", "e5m2"):
        byte = np.frexp(amax)[1] - 1 + 127 - (7 if fmt == "e4m3" else 14)
    else:
        mant, ex = np.frexp(amax / 6.0)
        byte = np.where(mant > 0.5, ex, ex - 1) + 127
    byte = np.clip(np.where(amax > 0, byte, 1), 1, 254)
    scaled = (w * np.exp2(127.0 - byte)[:, None, :]).reshape(k, n).astype(np.float32)
    by_word = np.ascontiguousarray(scaled.reshape(k // 512, 128, 4, n).transpose(0, 1, 3, 2))
    if fmt in ("e4m3", "e5m2"):
        words = by_word.astype(ml_dtypes.float8_e4m3fn if fmt == "e4m3" else ml_dtypes.float8_e5m2).view(np.uint8)
    else:
        c = by_word.astype(ml_dtypes.float4_e2m1fn).view(np.uint8) & 0xF
        words = (c[..., 0::2] | (c[..., 1::2] << 4)).reshape(k // 512, 128, 2 * n)
    return np.ascontiguousarray(words), np.ascontiguousarray(byte.astype(np.uint8).reshape(k // 512, 16, n))


def unpack_weight(words, scales, fmt):
    g, _, n = scales.shape
    words = np.ascontiguousarray(words).reshape(g, 128, n, -1)
    if fmt in ("e4m3", "e5m2"):
        vals = words.view(ml_dtypes.float8_e4m3fn if fmt == "e4m3" else ml_dtypes.float8_e5m2).astype(np.float64)
    else:
        nib = np.empty((g, 128, n, 4), np.uint8)
        nib[..., 0::2] = words & 0xF
        nib[..., 1::2] = words >> 4
        vals = E2M1[nib]
    vals = vals * np.repeat(np.exp2(scales.astype(np.float64) - 127.0), 8, axis=1)[..., None]
    return vals.transpose(0, 1, 3, 2).reshape(g * 512, n)


K, T, J, R, C, O, N, L, E = 512, 1024, 256, 512, 512, 256, 256, 512, 128


def setup_inputs():
    n = np.random.standard_normal
    idx = np.random.permutation(T)[:J]
    idx2 = np.random.permutation(C)[:J]
    idx3 = np.random.permutation(C)[:J]
    idx4 = np.random.permutation(C)[:O]
    idx5 = np.random.permutation(C)[:O]
    idx6 = np.random.permutation(O)[:E]
    idx7 = np.random.permutation(O)[:E]
    fk = mx_kscale(K)
    fr = mx_kscale(R)
    fl = mx_kscale(L)
    xtp = pack_weight(n((K, T)) / fk[:, None], "e5m2")
    wp = pack_weight(n((K, R)) * 1 / np.sqrt(K) * fk[:, None] * fr, "e2m1")
    w2p = pack_weight(n((K, R)) * 1 / np.sqrt(K) * fk[:, None] * fr, "e4m3")
    wbp = pack_weight(n((R, N)) * 1 / np.sqrt(R) / fr[:, None], "e2m1")
    sxp = pack_weight(n((L, O)) / fl[:, None], "e4m3")
    wsp = pack_weight(n((L, N)) * 1 / np.sqrt(L) * fl[:, None], "e2m1")
    return {
        "xt_words": xtp[0],
        "xt_scales": xtp[1],
        "w_words": wp[0],
        "w_scales": wp[1],
        "w2_words": w2p[0],
        "w2_scales": w2p[1],
        "wb_words": wbp[0],
        "wb_scales": wbp[1],
        "sx_words": sxp[0],
        "sx_scales": sxp[1],
        "ws_words": wsp[0],
        "ws_scales": wsp[1],
        "offs": striped(idx),
        "offs2": striped(idx2),
        "offs3": striped(idx3),
        "offs4": striped(idx4),
        "offs5": striped(idx5),
        "offs6": striped(idx6),
        "offs7": striped(idx7),
    }


def reference(xt_words, xt_scales, w_words, w_scales, w2_words, w2_scales, wb_words, wb_scales, sx_words, sx_scales, ws_words, ws_scales, offs, offs2, offs3, offs4, offs5, offs6, offs7):
    idx = unstriped(offs)
    idx2 = unstriped(offs2)
    idx3 = unstriped(offs3)
    idx4 = unstriped(offs4)
    idx5 = unstriped(offs5)
    idx6 = unstriped(offs6)
    idx7 = unstriped(offs7)
    xtu = unpack_weight(xt_words, xt_scales, "e5m2")
    wu = unpack_weight(w_words, w_scales, "e2m1")
    w2u = unpack_weight(w2_words, w2_scales, "e4m3")
    wbu = unpack_weight(wb_words, wb_scales, "e2m1")
    sxu = unpack_weight(sx_words, sx_scales, "e4m3")
    wsu = unpack_weight(ws_words, ws_scales, "e2m1")
    xtidxg = xtu[:, idx]
    a = wu.T @ xtidxg
    b = w2u.T @ xtidxg
    pw = np.zeros((R, C))
    pw[:, idx2] = a
    pv = np.zeros((R, C))
    pv[:, idx3] = b
    hid = np.abs(pw[:, idx4] - pv[:, idx5])
    hidq = mxq(hid, 0, "e4m3")
    p = wbu.T @ hidq + wsu.T @ sxu
    y = np.maximum(p[:, idx6], p[:, idx7])
    return y

@@ -1,0 +1,222 @@
+from contextlib import ExitStack
+
+import concourse.mybir as mybir
+
+K, T, J, R, C, O, N, L, E = 512, 1024, 256, 512, 512, 256, 256, 512, 128
+FLOPS = 2 * (2 * K * R * J + R * N * O + L * N * O)
+
+F32 = mybir.dt.float32
+BF16 = mybir.dt.bfloat16
+I32 = mybir.dt.int32
+U32 = mybir.dt.uint32
+U16 = mybir.dt.uint16
+U8 = mybir.dt.uint8
+E4M3 = mybir.dt.float8_e4m3fn_x4
+E5M2 = mybir.dt.float8_e5m2_x4
+E2M1 = mybir.dt.float4_e2m1fn_x4
+ACT = mybir.ActivationFunctionType
+ALU = mybir.AluOpType
+
+P = 128
+PACK = 4
+QUADS = 4
+
+
+def tile_list_twow_twoboards_skip_bestoftwo_kernel(
+    tc, xt_words, xt_scales, w_words, w_scales, w2_words, w2_scales, wb_words, wb_scales,
+    sx_words, sx_scales, ws_words, ws_scales, offs, offs2, offs3, offs4, offs5, offs6, offs7, out,
+):
+    nc = tc.nc
+    with ExitStack() as ctx:
+        lists = ctx.enter_context(tc.tile_pool(name="lists", bufs=1))
+        sb = ctx.enter_context(tc.tile_pool(name="sb", bufs=1))
+        ps = ctx.enter_context(tc.psum_pool(name="ps", bufs=1))
+
+        stage = ctx.enter_context(tc.tile_pool(name="stage", bufs=1))
+        board_bytes = 4 * C
+        places = {"xt_plane": 0, "w_raw": T, "xt_raw": board_bytes, "w2_raw": 3 * board_bytes,
+                  "pv0": 0, "pv1": board_bytes, "pv2": 2 * board_bytes, "pv3": 3 * board_bytes}
+
+        def tile(name, cols, dtype):
+            if name in places:
+                return stage.tile([P, cols], dtype, name=name, align_bytes=64, offset=places[name])
+            return sb.tile([P, cols], dtype, name=name, align_bytes=64)
+
+        def load_list(name, src):
+            t = lists.tile([P, src.shape[1]], U16, name=name)
+            nc.sync.dma_start(t[:], src)
+            return t
+
+        def load_words8(queue, name, src, cols):
+            t = tile(name, cols, U32)
+            queue.dma_start(t[:].bitcast(I32), src[0].rearrange("p n t -> p (n t)").bitcast(I32))
+            return t
+
+        def load_words4(queue, name, src, cols):
+            t = tile(name, cols, U16)
+            queue.dma_start(t[:].bitcast(I32), src[0].bitcast(I32))
+            return t
+
+        def zero_plane(name, cols):
+            t = tile(name, cols, U8)
+            nc.vector.memset(t[:].bitcast(I32), 0)
+            return t
+
+        def load_plane(queue, t, src, quads):
+            for q in quads:
+                queue.dma_start(t[32 * q : 32 * q + 4, :].bitcast(I32), src[0, 4 * q : 4 * q + 4, :].bitcast(I32))
+
+        xt_plane = zero_plane("xt_plane", T)
+        w_plane = zero_plane("w_plane", R)
+        w2_plane = zero_plane("w2_plane", R)
+        pw = [tile("pw%d" % t, C, F32) for t in range(PACK)]
+        pv = [tile("pv%d" % t, C, F32) for t in range(PACK)]
+        for board in pw:
+            nc.vector.memset(board[:].bitcast(I32), 0)
+        ws_plane = tile("ws_plane", N, U8)
+        sx_plane = tile("sx_plane", O, U8)
+        wb_plane = tile("wb_plane", N, U8)
+
+        o1 = load_list("o1", offs)
+        o2 = load_list("o2", offs2)
+        w_raw = load_words4(nc.sync, "w_raw", w_words, R)
+        load_plane(nc.sync, xt_plane, xt_scales, range(QUADS))
+        xt_raw = load_words8(nc.sync, "xt_raw", xt_words, T)
+        load_plane(nc.sync, w_plane, w_scales, range(QUADS))
+        w2_raw = load_words8(nc.sync, "w2_raw", w2_words, R)
+        load_plane(nc.sync, w2_plane, w2_scales, range(QUADS))
+        o3 = load_list("o3", offs3)
+        o4 = load_list("o4", offs4)
+        o5 = load_list("o5", offs5)
+        ws_q = load_words4(nc.sync, "ws_q", ws_words, N)
+        sx_q = load_words8(nc.sync, "sx_q", sx_words, O)
+        wb_q = load_words4(nc.sync, "wb_q", wb_words, N)
+        load_plane(nc.sync, ws_plane, ws_scales, range(QUADS))
+        load_plane(nc.sync, sx_plane, sx_scales, range(QUADS))
+        load_plane(nc.sync, wb_plane, wb_scales, range(QUADS))
+        o6 = load_list("o6", offs6)
+        o7 = load_list("o7", offs7)
+
+        xg_plane = tile("xg_plane", J, U8)
+        nc.vector.tensor_copy(xg_plane[:], xt_plane[:].indirect(o1[:]))
+        w_q = tile("w_q", R, U16)
+        nc.scalar.copy(w_q[:].rearrange("p (t m) -> p t m", t=PACK), w_raw[:].rearrange("p (m t) -> p t m", t=PACK))
+        xg_q = tile("xg_q", J, U32)
+        nc.vector.tensor_copy(xg_q[:], xt_raw[:].indirect(o1[:]))
+        w_sc = tile("w_sc", R, U8)
+        nc.vector.tensor_copy(w_sc[:].rearrange("p (t m) -> p t m", t=PACK), w_plane[:].rearrange("p (m t) -> p t m", t=PACK))
+
+        for board in pv[:3]:
+            nc.gpsimd.memset(board[:], 0.0)
+
+        bank_a0 = ps.tile([P, J], F32, name="bank_a0")
+        bank_a1 = ps.tile([P, J], F32, name="bank_a1")
+        bank_a23 = ps.tile([P, 2 * J], F32, name="bank_a23")
+        bank_b0 = ps.tile([P, J], F32, name="bank_b0")
+        bank_b1 = ps.tile([P, J], F32, name="bank_b1")
+        bank_b23 = ps.tile([P, 2 * J], F32, name="bank_b23")
+        a_ps = [bank_a0[:], bank_a1[:], bank_a23[:, 0:J], bank_a23[:, J : 2 * J]]
+        b_ps = [bank_b0[:], bank_b1[:], bank_b23[:, 0:J], bank_b23[:, J : 2 * J]]
+
+        def first_stage(dst, words, scales, fmt, t):
+            cols = slice(t * P, (t + 1) * P)
+            nc.tensor.matmul_mx(out=dst, lhsT=words[:, cols].bitcast(fmt), lhsT_scale=scales[:, cols],
+                                rhs=xg_q[:].bitcast(E5M2), rhs_scale=xg_plane[:], start=True, stop=True)
+
+        for t in range(PACK):
+            first_stage(a_ps[t], w_q, w_sc, E2M1, t)
+
+        a0 = tile("a0", J, F32)
+        a1 = tile("a1", J, F32)
+        a23 = tile("a23", 2 * J, F32)
+        b0 = tile("b0", J, F32)
+        b1 = tile("b1", J, F32)
+        b23 = tile("b23", 2 * J, F32)
+
+        nc.vector.tensor_copy(a0[:], bank_a0[:])
+        nc.scalar.copy(a1[:], bank_a1[:])
+        nc.scalar.activation(pw[1][:].indirect(o2[:]), a1[:], ACT.Copy)
+
+        w2_q = tile("w2_q", R, U32)
+        nc.scalar.copy(w2_q[:].rearrange("p (t m) -> p m t", t=PACK), w2_raw[:].rearrange("p (m t) -> p m t", t=PACK))
+        w2_sc = tile("w2_sc", R, U8)
+        nc.gpsimd.tensor_copy(w2_sc[:].rearrange("p (t m) -> p t m", t=PACK), w2_plane[:].rearrange("p (m t) -> p t m", t=PACK))
+        nc.gpsimd.memset(pv[3][:], 0.0)
+        for t in range(PACK):
+            first_stage(b_ps[t], w2_q, w2_sc, E4M3, t)
+
+        nc.vector.tensor_copy(pw[0][:].indirect(o2[:]), a0[:])
+        nc.scalar.copy(b0[:], bank_b0[:])
+        nc.vector.tensor_copy(b1[:], bank_b1[:])
+        nc.scalar.activation(pv[0][:].indirect(o3[:]), b0[:], ACT.Copy)
+        nc.vector.tensor_copy(pv[1][:].indirect(o3[:]), b1[:])
+
+        picked = [tile("picked%d" % t, O, F32) for t in range(PACK)]
+        diff01 = tile("diff01", 2 * O, F32)
+        diff23 = tile("diff23", 2 * O, F32)
+        diff = [diff01[:, 0:O], diff01[:, O : 2 * O], diff23[:, 0:O], diff23[:, O : 2 * O]]
+
+        nc.scalar.activation(picked[1][:], pw[1][:].indirect(o4[:]), ACT.Copy)
+        nc.scalar.activation(picked[0][:], pv[0][:].indirect(o5[:]), ACT.Copy)
+        nc.vector.tensor_copy(a23[:], bank_a23[:])
+        nc.scalar.copy(b23[:], bank_b23[:])
+        nc.vector.tensor_copy(pw[2][:].indirect(o2[:]), a23[:, 0:J])
+        nc.scalar.activation(pv[2][:].indirect(o3[:]), b23[:, 0:J], ACT.Copy)
+        nc.vector.tensor_tensor(diff[1], pv[1][:].indirect(o5[:]), picked[1][:], ALU.subtract)
+        nc.vector.tensor_tensor(diff[0], pw[0][:].indirect(o4[:]), picked[0][:], ALU.subtract)
+        nc.scalar.activation(pv[3][:].indirect(o3[:]), b23[:, J : 2 * J], ACT.Copy)
+        nc.vector.tensor_copy(pw[3][:].indirect(o2[:]), a23[:, J : 2 * J])
+        nc.scalar.activation(picked[2][:], pv[2][:].indirect(o5[:]), ACT.Copy)
+        nc.scalar.activation(picked[3][:], pv[3][:].indirect(o5[:]), ACT.Copy)
+        half = O // 2
+        pairs = [tile("pairs%d" % h, PACK * half, BF16) for h in range(2)]
+
+        def magnitudes(h, which, src):
+            dst = pairs[h][:, which * 2 * half : (which + 1) * 2 * half].rearrange("p (o u) -> p o u", u=2)
+            nc.scalar.activation(dst, src[:].rearrange("p (u o) -> p o u", u=2)[:, h * half : (h + 1) * half, :], ACT.Abs)
+
+        for h in range(2):
+            magnitudes(h, 0, diff01)
+        nc.vector.tensor_tensor(diff[2], pw[2][:].indirect(o4[:]), picked[2][:], ALU.subtract)
+        for h in range(2):
+            reads = slice(h * half, (h + 1) * half)
+            nc.vector.tensor_tensor(diff[3][:, reads], pw[3][:].indirect(o4[:, h * half // 16 : (h + 1) * half // 16]),
+                                    picked[3][:, reads], ALU.subtract)
+            magnitudes(h, 1, diff23)
+
+        banks_p = [ps.tile([P, O], F32, name="bank_p%d" % nt) for nt in range(N // P)]
+        for nt in range(N // P):
+            cols = slice(nt * P, (nt + 1) * P)
+            nc.tensor.matmul_mx(out=banks_p[nt][:], lhsT=ws_q[:, cols].bitcast(E2M1), lhsT_scale=ws_plane[:, cols],
+                                rhs=sx_q[:].bitcast(E4M3), rhs_scale=sx_plane[:], start=True, stop=False)
+        hid = [tile("hid%d" % h, PACK * half, BF16) for h in range(2)]
+        for h in range(2):
+            nc.vector.tensor_copy(hid[h][:].bitcast(I32).rearrange("p (o w) -> p o w", w=2),
+                                  pairs[h][:].bitcast(I32).rearrange("p (w o) -> p o w", w=2))
+        for h in range(2):
+            hid_q = tile("hid_q%d" % h, half, U32)
+            hid_sc = tile("hid_sc%d" % h, half, U8)
+            nc.vector.quantize_mx(out=hid_q[:].bitcast(E4M3), scales=hid_sc[:], in_=hid[h][:])
+            for nt in range(N // P):
+                cols = slice(nt * P, (nt + 1) * P)
+                nc.tensor.matmul_mx(out=banks_p[nt][:, h * half : (h + 1) * half], lhsT=wb_q[:, cols].bitcast(E2M1),
+                                    lhsT_scale=wb_plane[:, cols], rhs=hid_q[:].bitcast(E4M3), rhs_scale=hid_sc[:],
+                                    start=False, stop=(h == 1))
+
+        for nt in range(N // P):
+            cols = slice(nt * P, (nt + 1) * P)
+            bank_p = banks_p[nt]
+            p_sb = tile("p_sb%d" % nt, O, F32)
+            first = tile("first%d" % nt, E, F32)
+            second = tile("second%d" % nt, E, F32)
+            best = tile("best%d" % nt, E, F32)
+            if nt == 0:
+                nc.vector.tensor_copy(p_sb[:], bank_p[:])
+                nc.vector.tensor_copy(first[:], p_sb[:].indirect(o6[:]))
+                nc.vector.tensor_copy(second[:], p_sb[:].indirect(o7[:]))
+            else:
+                nc.scalar.copy(p_sb[:], bank_p[:])
+                nc.scalar.activation(first[:], p_sb[:].indirect(o6[:]), ACT.Copy)
+                nc.scalar.activation(second[:], p_sb[:].indirect(o7[:]), ACT.Copy)
+            nc.vector.tensor_tensor(best[:], first[:], second[:], ALU.max)
+            nc.sync.dma_start(out[cols, :], best[:])

@@ -34,7 +34,7 @@ def tile_list_twow_twoboards_skip_bestoftwo_kernel(
 
         stage = ctx.enter_context(tc.tile_pool(name="stage", bufs=1))
         board_bytes = 4 * C
-        places = {"xt_plane": 0, "w_raw": T, "xt_raw": board_bytes, "w2_raw": 3 * board_bytes,
+        places = {"xt_raw": 0, "xt_plane": 2 * board_bytes, "w_raw": 2 * board_bytes + T, "w2_raw": 3 * board_bytes,
                   "pv0": 0, "pv1": board_bytes, "pv2": 2 * board_bytes, "pv3": 3 * board_bytes}
 
         def tile(name, cols, dtype):
@@ -71,19 +71,20 @@ def tile_list_twow_twoboards_skip_bestoftwo_kernel(
         w2_plane = zero_plane("w2_plane", R)
         pw = [tile("pw%d" % t, C, F32) for t in range(PACK)]
         pv = [tile("pv%d" % t, C, F32) for t in range(PACK)]
-        for board in pw:
-            nc.vector.memset(board[:].bitcast(I32), 0)
+        for board in (pw[1], pw[0], pw[2], pw[3]):
+            nc.vector.memset(board[:], 0.0)
         ws_plane = tile("ws_plane", N, U8)
         sx_plane = tile("sx_plane", O, U8)
         wb_plane = tile("wb_plane", N, U8)
 
+        w_rows = sb.tile([4, QUADS, R // 4], I32, name="w_rows", align_bytes=64)
+        nc.sync.dma_start(w_rows[:], w_scales[0].bitcast(I32).rearrange("(q r) c -> r q c", q=QUADS))
         o1 = load_list("o1", offs)
-        o2 = load_list("o2", offs2)
+        xt_raw = load_words8(nc.sync, "xt_raw", xt_words, T)
         w_raw = load_words4(nc.sync, "w_raw", w_words, R)
         load_plane(nc.sync, xt_plane, xt_scales, range(QUADS))
-        xt_raw = load_words8(nc.sync, "xt_raw", xt_words, T)
-        load_plane(nc.sync, w_plane, w_scales, range(QUADS))
         w2_raw = load_words8(nc.sync, "w2_raw", w2_words, R)
+        o2 = load_list("o2", offs2)
         load_plane(nc.sync, w2_plane, w2_scales, range(QUADS))
         o3 = load_list("o3", offs3)
         o4 = load_list("o4", offs4)
@@ -97,20 +98,23 @@ def tile_list_twow_twoboards_skip_bestoftwo_kernel(
         o6 = load_list("o6", offs6)
         o7 = load_list("o7", offs7)
 
-        xg_plane = tile("xg_plane", J, U8)
-        nc.vector.tensor_copy(xg_plane[:], xt_plane[:].indirect(o1[:]))
+        for q in range(QUADS):
+            nc.vector.tensor_copy(w_plane[32 * q : 32 * q + 4, :].bitcast(I32), w_rows[:, q, :])
+        w_sc = tile("w_sc", R, U8)
+        nc.vector.tensor_copy(w_sc[:].rearrange("p (t m) -> p t m", t=PACK), w_plane[:].rearrange("p (m t) -> p t m", t=PACK))
         w_q = tile("w_q", R, U16)
         nc.scalar.copy(w_q[:].rearrange("p (t m) -> p t m", t=PACK), w_raw[:].rearrange("p (m t) -> p t m", t=PACK))
         xg_q = tile("xg_q", J, U32)
         nc.vector.tensor_copy(xg_q[:], xt_raw[:].indirect(o1[:]))
-        w_sc = tile("w_sc", R, U8)
-        nc.vector.tensor_copy(w_sc[:].rearrange("p (t m) -> p t m", t=PACK), w_plane[:].rearrange("p (m t) -> p t m", t=PACK))
+        xg_plane = tile("xg_plane", J, U8)
+        for h in range(2):
+            nc.vector.tensor_copy(xg_plane[:, h * P : (h + 1) * P], xt_plane[:].indirect(o1[:, h * P // 16 : (h + 1) * P // 16]))
 
-        for board in pv[:3]:
-            nc.gpsimd.memset(board[:], 0.0)
+        w2_q = tile("w2_q", R, U32)
+        nc.vector.tensor_copy(w2_q[:].rearrange("p (t m) -> p m t", t=PACK), w2_raw[:].rearrange("p (m t) -> p m t", t=PACK))
 
-        bank_a0 = ps.tile([P, J], F32, name="bank_a0")
-        bank_a1 = ps.tile([P, J], F32, name="bank_a1")
+        bank_a0 = ps.tile([P, J], F32, name="bank_a0", tag="bank_a0")
+        bank_a1 = ps.tile([P, J], F32, name="bank_a1", tag="bank_a1")
         bank_a23 = ps.tile([P, 2 * J], F32, name="bank_a23")
         bank_b0 = ps.tile([P, J], F32, name="bank_b0")
         bank_b1 = ps.tile([P, J], F32, name="bank_b1")
@@ -118,30 +122,34 @@ def tile_list_twow_twoboards_skip_bestoftwo_kernel(
         a_ps = [bank_a0[:], bank_a1[:], bank_a23[:, 0:J], bank_a23[:, J : 2 * J]]
         b_ps = [bank_b0[:], bank_b1[:], bank_b23[:, 0:J], bank_b23[:, J : 2 * J]]
 
-        def first_stage(dst, words, scales, fmt, t):
+        def first_stage(dst, words, scales, fmt, t, slots=slice(0, J)):
             cols = slice(t * P, (t + 1) * P)
-            nc.tensor.matmul_mx(out=dst, lhsT=words[:, cols].bitcast(fmt), lhsT_scale=scales[:, cols],
-                                rhs=xg_q[:].bitcast(E5M2), rhs_scale=xg_plane[:], start=True, stop=True)
+            nc.tensor.matmul_mx(out=dst[:, slots], lhsT=words[:, cols].bitcast(fmt), lhsT_scale=scales[:, cols],
+                                rhs=xg_q[:, slots].bitcast(E5M2), rhs_scale=xg_plane[:, slots], start=True, stop=True)
 
-        for t in range(PACK):
-            first_stage(a_ps[t], w_q, w_sc, E2M1, t)
+        a1 = tile("a1", J, F32)
+        first_stage(a_ps[1], w_q, w_sc, E2M1, 1, slice(0, P))
+        nc.scalar.copy(a1[:, 0:P], bank_a1[:, 0:P])
+        nc.scalar.activation(pw[1][:].indirect(o2[:, 0 : P // 16]), a1[:, 0:P], ACT.Copy)
+        first_stage(a_ps[0], w_q, w_sc, E2M1, 0)
+        first_stage(a_ps[1], w_q, w_sc, E2M1, 1, slice(P, J))
+        first_stage(a_ps[2], w_q, w_sc, E2M1, 2)
+        first_stage(a_ps[3], w_q, w_sc, E2M1, 3)
 
         a0 = tile("a0", J, F32)
-        a1 = tile("a1", J, F32)
         a23 = tile("a23", 2 * J, F32)
         b0 = tile("b0", J, F32)
         b1 = tile("b1", J, F32)
         b23 = tile("b23", 2 * J, F32)
 
         nc.vector.tensor_copy(a0[:], bank_a0[:])
-        nc.scalar.copy(a1[:], bank_a1[:])
-        nc.scalar.activation(pw[1][:].indirect(o2[:]), a1[:], ACT.Copy)
+        nc.scalar.copy(a1[:, P:J], bank_a1[:, P:J])
+        nc.scalar.activation(pw[1][:].indirect(o2[:, P // 16 : J // 16]), a1[:, P:J], ACT.Copy)
 
-        w2_q = tile("w2_q", R, U32)
-        nc.scalar.copy(w2_q[:].rearrange("p (t m) -> p m t", t=PACK), w2_raw[:].rearrange("p (m t) -> p m t", t=PACK))
         w2_sc = tile("w2_sc", R, U8)
         nc.gpsimd.tensor_copy(w2_sc[:].rearrange("p (t m) -> p t m", t=PACK), w2_plane[:].rearrange("p (m t) -> p t m", t=PACK))
-        nc.gpsimd.memset(pv[3][:], 0.0)
+        for board in pv:
+            nc.gpsimd.memset(board[:], 0.0)
         for t in range(PACK):
             first_stage(b_ps[t], w2_q, w2_sc, E4M3, t)
 
@@ -184,11 +192,16 @@ def tile_list_twow_twoboards_skip_bestoftwo_kernel(
                                     picked[3][:, reads], ALU.subtract)
             magnitudes(h, 1, diff23)
 
-        banks_p = [ps.tile([P, O], F32, name="bank_p%d" % nt) for nt in range(N // P)]
-        for nt in range(N // P):
-            cols = slice(nt * P, (nt + 1) * P)
-            nc.tensor.matmul_mx(out=banks_p[nt][:], lhsT=ws_q[:, cols].bitcast(E2M1), lhsT_scale=ws_plane[:, cols],
-                                rhs=sx_q[:].bitcast(E4M3), rhs_scale=sx_plane[:], start=True, stop=False)
+        reuse = {(0, 0): "bank_a0", (0, 1): "bank_a1", (1, 0): "bank_p0", (1, 1): "bank_p1"}
+        banks_p = {}
+        for h in range(2):
+            reads = slice(h * half, (h + 1) * half)
+            for nt in range(N // P):
+                cols = slice(nt * P, (nt + 1) * P)
+                banks_p[h, nt] = ps.tile([P, half], F32, name="p_%d_%d" % (h, nt), tag=reuse[h, nt])
+                nc.tensor.matmul_mx(out=banks_p[h, nt][:], lhsT=ws_q[:, cols].bitcast(E2M1), lhsT_scale=ws_plane[:, cols],
+                                    rhs=sx_q[:, reads].bitcast(E4M3), rhs_scale=sx_plane[:, reads], start=True, stop=False)
+        p_sb = [tile("p_sb%d" % nt, O, F32) for nt in range(N // P)]
         hid = [tile("hid%d" % h, PACK * half, BF16) for h in range(2)]
         for h in range(2):
             nc.vector.tensor_copy(hid[h][:].bitcast(I32).rearrange("p (o w) -> p o w", w=2),
@@ -197,26 +210,23 @@ def tile_list_twow_twoboards_skip_bestoftwo_kernel(
             hid_q = tile("hid_q%d" % h, half, U32)
             hid_sc = tile("hid_sc%d" % h, half, U8)
             nc.vector.quantize_mx(out=hid_q[:].bitcast(E4M3), scales=hid_sc[:], in_=hid[h][:])
-            for nt in range(N // P):
+            for nt in (1, 0):
                 cols = slice(nt * P, (nt + 1) * P)
-                nc.tensor.matmul_mx(out=banks_p[nt][:, h * half : (h + 1) * half], lhsT=wb_q[:, cols].bitcast(E2M1),
+                nc.tensor.matmul_mx(out=banks_p[h, nt][:], lhsT=wb_q[:, cols].bitcast(E2M1),
                                     lhsT_scale=wb_plane[:, cols], rhs=hid_q[:].bitcast(E4M3), rhs_scale=hid_sc[:],
-                                    start=False, stop=(h == 1))
+                                    start=False, stop=True)
+                if h == 1 and nt == 0:
+                    nc.vector.tensor_copy(p_sb[nt][:, half:O], banks_p[h, nt][:])
+                else:
+                    nc.scalar.copy(p_sb[nt][:, h * half : (h + 1) * half], banks_p[h, nt][:])
 
-        for nt in range(N // P):
-            cols = slice(nt * P, (nt + 1) * P)
-            bank_p = banks_p[nt]
-            p_sb = tile("p_sb%d" % nt, O, F32)
-            first = tile("first%d" % nt, E, F32)
-            second = tile("second%d" % nt, E, F32)
+        first = [tile("first%d" % nt, E, F32) for nt in range(N // P)]
+        second = [tile("second%d" % nt, E, F32) for nt in range(N // P)]
+        nc.scalar.activation(first[1][:], p_sb[1][:].indirect(o6[:]), ACT.Copy)
+        nc.scalar.activation(second[1][:], p_sb[1][:].indirect(o7[:]), ACT.Copy)
+        nc.vector.tensor_copy(first[0][:], p_sb[0][:].indirect(o6[:]))
+        nc.vector.tensor_copy(second[0][:], p_sb[0][:].indirect(o7[:]))
+        for nt in (1, 0):
             best = tile("best%d" % nt, E, F32)
-            if nt == 0:
-                nc.vector.tensor_copy(p_sb[:], bank_p[:])
-                nc.vector.tensor_copy(first[:], p_sb[:].indirect(o6[:]))
-                nc.vector.tensor_copy(second[:], p_sb[:].indirect(o7[:]))
-            else:
-                nc.scalar.copy(p_sb[:], bank_p[:])
-                nc.scalar.activation(first[:], p_sb[:].indirect(o6[:]), ACT.Copy)
-                nc.scalar.activation(second[:], p_sb[:].indirect(o7[:]), ACT.Copy)
-            nc.vector.tensor_tensor(best[:], first[:], second[:], ALU.max)
-            nc.sync.dma_start(out[cols, :], best[:])
+            nc.vector.tensor_tensor(best[:], first[nt][:], second[nt][:], ALU.max)
+            nc.sync.dma_start(out[nt * P : (nt + 1) * P, :], best[:])

@@ -34,8 +34,11 @@ def tile_list_twow_twoboards_skip_bestoftwo_kernel(
 
         stage = ctx.enter_context(tc.tile_pool(name="stage", bufs=1))
         board_bytes = 4 * C
-        places = {"xt_raw": 0, "xt_plane": 2 * board_bytes, "w_raw": 2 * board_bytes + T, "w2_raw": 3 * board_bytes,
-                  "pv0": 0, "pv1": board_bytes, "pv2": 2 * board_bytes, "pv3": 3 * board_bytes}
+        places = {"w_plane": 0, "xt_raw": board_bytes, "xt_plane": 3 * board_bytes, "w_raw": 3 * board_bytes + T,
+                  "w2_plane": 4 * board_bytes, "w2_sc": 5 * board_bytes,
+                  "pw2": 0, "pw3": board_bytes, "pv1": 2 * board_bytes, "pv0": 3 * board_bytes,
+                  "pv3": 4 * board_bytes, "pv2": 5 * board_bytes,
+                  "w2_q": 6 * board_bytes, "from_pw3": 6 * board_bytes}
 
         def tile(name, cols, dtype):
             if name in places:
@@ -71,7 +74,7 @@ def tile_list_twow_twoboards_skip_bestoftwo_kernel(
         w2_plane = zero_plane("w2_plane", R)
         pw = [tile("pw%d" % t, C, F32) for t in range(PACK)]
         pv = [tile("pv%d" % t, C, F32) for t in range(PACK)]
-        for board in (pw[1], pw[0], pw[2], pw[3]):
+        for board in (pw[0], pw[1]):
             nc.vector.memset(board[:], 0.0)
         ws_plane = tile("ws_plane", N, U8)
         sx_plane = tile("sx_plane", O, U8)
@@ -102,110 +105,80 @@ def tile_list_twow_twoboards_skip_bestoftwo_kernel(
             nc.vector.tensor_copy(w_plane[32 * q : 32 * q + 4, :].bitcast(I32), w_rows[:, q, :])
         w_sc = tile("w_sc", R, U8)
         nc.vector.tensor_copy(w_sc[:].rearrange("p (t m) -> p t m", t=PACK), w_plane[:].rearrange("p (m t) -> p t m", t=PACK))
+        nc.gpsimd.memset(pw[2][:], 0.0)
         w_q = tile("w_q", R, U16)
         nc.scalar.copy(w_q[:].rearrange("p (t m) -> p t m", t=PACK), w_raw[:].rearrange("p (m t) -> p t m", t=PACK))
         xg_q = tile("xg_q", J, U32)
         nc.vector.tensor_copy(xg_q[:], xt_raw[:].indirect(o1[:]))
         xg_plane = tile("xg_plane", J, U8)
-        for h in range(2):
-            nc.vector.tensor_copy(xg_plane[:, h * P : (h + 1) * P], xt_plane[:].indirect(o1[:, h * P // 16 : (h + 1) * P // 16]))
+        nc.vector.tensor_copy(xg_plane[:], xt_plane[:].indirect(o1[:]))
 
         w2_q = tile("w2_q", R, U32)
         nc.vector.tensor_copy(w2_q[:].rearrange("p (t m) -> p m t", t=PACK), w2_raw[:].rearrange("p (m t) -> p m t", t=PACK))
 
-        bank_a0 = ps.tile([P, J], F32, name="bank_a0", tag="bank_a0")
-        bank_a1 = ps.tile([P, J], F32, name="bank_a1", tag="bank_a1")
-        bank_a23 = ps.tile([P, 2 * J], F32, name="bank_a23")
-        bank_b0 = ps.tile([P, J], F32, name="bank_b0")
-        bank_b1 = ps.tile([P, J], F32, name="bank_b1")
-        bank_b23 = ps.tile([P, 2 * J], F32, name="bank_b23")
-        a_ps = [bank_a0[:], bank_a1[:], bank_a23[:, 0:J], bank_a23[:, J : 2 * J]]
-        b_ps = [bank_b0[:], bank_b1[:], bank_b23[:, 0:J], bank_b23[:, J : 2 * J]]
-
-        def first_stage(dst, words, scales, fmt, t, slots=slice(0, J)):
+        def first_stage(dst, words, scales, fmt, t):
             cols = slice(t * P, (t + 1) * P)
-            nc.tensor.matmul_mx(out=dst[:, slots], lhsT=words[:, cols].bitcast(fmt), lhsT_scale=scales[:, cols],
-                                rhs=xg_q[:, slots].bitcast(E5M2), rhs_scale=xg_plane[:, slots], start=True, stop=True)
+            nc.tensor.matmul_mx(out=dst, lhsT=words[:, cols].bitcast(fmt), lhsT_scale=scales[:, cols],
+                                rhs=xg_q[:].bitcast(E5M2), rhs_scale=xg_plane[:], start=True, stop=True)
 
-        a1 = tile("a1", J, F32)
-        first_stage(a_ps[1], w_q, w_sc, E2M1, 1, slice(0, P))
-        nc.scalar.copy(a1[:, 0:P], bank_a1[:, 0:P])
-        nc.scalar.activation(pw[1][:].indirect(o2[:, 0 : P // 16]), a1[:, 0:P], ACT.Copy)
-        first_stage(a_ps[0], w_q, w_sc, E2M1, 0)
-        first_stage(a_ps[1], w_q, w_sc, E2M1, 1, slice(P, J))
-        first_stage(a_ps[2], w_q, w_sc, E2M1, 2)
-        first_stage(a_ps[3], w_q, w_sc, E2M1, 3)
-
-        a0 = tile("a0", J, F32)
-        a23 = tile("a23", 2 * J, F32)
-        b0 = tile("b0", J, F32)
-        b1 = tile("b1", J, F32)
-        b23 = tile("b23", 2 * J, F32)
-
-        nc.vector.tensor_copy(a0[:], bank_a0[:])
-        nc.scalar.copy(a1[:, P:J], bank_a1[:, P:J])
-        nc.scalar.activation(pw[1][:].indirect(o2[:, P // 16 : J // 16]), a1[:, P:J], ACT.Copy)
-
+        a_ps = [ps.tile([P, J], F32, name="a_ps%d" % t, tag="bank_a%d" % t) for t in range(PACK)]
+        b_ps = [ps.tile([P, 2 * J], F32, name="b_ps%d" % u) for u in range(2)]
+        for t in range(PACK):
+            first_stage(a_ps[t][:], w_q, w_sc, E2M1, t)
         w2_sc = tile("w2_sc", R, U8)
         nc.gpsimd.tensor_copy(w2_sc[:].rearrange("p (t m) -> p t m", t=PACK), w2_plane[:].rearrange("p (m t) -> p t m", t=PACK))
-        for board in pv:
-            nc.gpsimd.memset(board[:], 0.0)
         for t in range(PACK):
-            first_stage(b_ps[t], w2_q, w2_sc, E4M3, t)
+            first_stage(b_ps[t // 2][:, (t % 2) * J : (t % 2 + 1) * J], w2_q, w2_sc, E4M3, t)
+        for board in (pw[3], pv[1], pv[0], pv[3], pv[2]):
+            nc.gpsimd.memset(board[:], 0.0)
 
-        nc.vector.tensor_copy(pw[0][:].indirect(o2[:]), a0[:])
-        nc.scalar.copy(b0[:], bank_b0[:])
-        nc.vector.tensor_copy(b1[:], bank_b1[:])
-        nc.scalar.activation(pv[0][:].indirect(o3[:]), b0[:], ACT.Copy)
-        nc.vector.tensor_copy(pv[1][:].indirect(o3[:]), b1[:])
+        a_sb = [tile("a%d" % t, J, F32) for t in range(PACK)]
+        b_sb = [tile("b%d" % u, 2 * J, F32) for u in range(2)]
+        from_pw = {t: tile("from_pw%d" % t, O, F32) for t in (0, 1, 3)}
+        from_pv = {t: tile("from_pv%d" % t, O, F32) for t in (0, 1, 2)}
+        diff_all = tile("diff", PACK * O, F32)
+        diff = [diff_all[:, t * O : (t + 1) * O] for t in range(PACK)]
 
-        picked = [tile("picked%d" % t, O, F32) for t in range(PACK)]
-        diff01 = tile("diff01", 2 * O, F32)
-        diff23 = tile("diff23", 2 * O, F32)
-        diff = [diff01[:, 0:O], diff01[:, O : 2 * O], diff23[:, 0:O], diff23[:, O : 2 * O]]
-
-        nc.scalar.activation(picked[1][:], pw[1][:].indirect(o4[:]), ACT.Copy)
-        nc.scalar.activation(picked[0][:], pv[0][:].indirect(o5[:]), ACT.Copy)
-        nc.vector.tensor_copy(a23[:], bank_a23[:])
-        nc.scalar.copy(b23[:], bank_b23[:])
-        nc.vector.tensor_copy(pw[2][:].indirect(o2[:]), a23[:, 0:J])
-        nc.scalar.activation(pv[2][:].indirect(o3[:]), b23[:, 0:J], ACT.Copy)
-        nc.vector.tensor_tensor(diff[1], pv[1][:].indirect(o5[:]), picked[1][:], ALU.subtract)
-        nc.vector.tensor_tensor(diff[0], pw[0][:].indirect(o4[:]), picked[0][:], ALU.subtract)
-        nc.scalar.activation(pv[3][:].indirect(o3[:]), b23[:, J : 2 * J], ACT.Copy)
-        nc.vector.tensor_copy(pw[3][:].indirect(o2[:]), a23[:, J : 2 * J])
-        nc.scalar.activation(picked[2][:], pv[2][:].indirect(o5[:]), ACT.Copy)
-        nc.scalar.activation(picked[3][:], pv[3][:].indirect(o5[:]), ACT.Copy)
+        for t in (0, 2):
+            nc.vector.tensor_copy(a_sb[t][:], a_ps[t][:])
+            nc.scalar.copy(a_sb[t + 1][:], a_ps[t + 1][:])
+        for t in (0, 2):
+            nc.vector.tensor_copy(pw[t][:].indirect(o2[:]), a_sb[t][:])
+            nc.scalar.activation(pw[t + 1][:].indirect(o2[:]), a_sb[t + 1][:], ACT.Copy)
+        nc.scalar.activation(from_pw[1][:], pw[1][:].indirect(o4[:]), ACT.Copy)
+        nc.vector.tensor_copy(from_pw[0][:], pw[0][:].indirect(o4[:]))
+        nc.vector.tensor_copy(b_sb[0][:], b_ps[0][:])
+        nc.scalar.activation(pv[0][:].indirect(o3[:]), b_sb[0][:, 0:J], ACT.Copy)
+        nc.vector.tensor_copy(pv[1][:].indirect(o3[:]), b_sb[0][:, J : 2 * J])
+        nc.scalar.copy(b_sb[1][:], b_ps[1][:])
+        nc.scalar.activation(from_pw[3][:], pw[3][:].indirect(o4[:]), ACT.Copy)
+        nc.scalar.activation(from_pv[0][:], pv[0][:].indirect(o5[:]), ACT.Copy)
+        nc.vector.tensor_copy(from_pv[1][:], pv[1][:].indirect(o5[:]))
+        nc.scalar.activation(pv[2][:].indirect(o3[:]), b_sb[1][:, 0:J], ACT.Copy)
+        nc.vector.tensor_copy(pv[3][:].indirect(o3[:]), b_sb[1][:, J : 2 * J])
+        for t in (1, 0):
+            nc.gpsimd.tensor_tensor(diff[t], from_pw[t][:], from_pv[t][:], ALU.subtract)
+        nc.vector.tensor_tensor(diff[3], pv[3][:].indirect(o5[:]), from_pw[3][:], ALU.subtract)
         half = O // 2
-        pairs = [tile("pairs%d" % h, PACK * half, BF16) for h in range(2)]
-
-        def magnitudes(h, which, src):
-            dst = pairs[h][:, which * 2 * half : (which + 1) * 2 * half].rearrange("p (o u) -> p o u", u=2)
-            nc.scalar.activation(dst, src[:].rearrange("p (u o) -> p o u", u=2)[:, h * half : (h + 1) * half, :], ACT.Abs)
-
-        for h in range(2):
-            magnitudes(h, 0, diff01)
-        nc.vector.tensor_tensor(diff[2], pw[2][:].indirect(o4[:]), picked[2][:], ALU.subtract)
+        hid = [tile("hid%d" % h, PACK * half, BF16) for h in range(2)]
         for h in range(2):
             reads = slice(h * half, (h + 1) * half)
-            nc.vector.tensor_tensor(diff[3][:, reads], pw[3][:].indirect(o4[:, h * half // 16 : (h + 1) * half // 16]),
-                                    picked[3][:, reads], ALU.subtract)
-            magnitudes(h, 1, diff23)
+            entries = slice(h * half // 16, (h + 1) * half // 16)
+            nc.scalar.activation(from_pv[2][:, reads], pv[2][:].indirect(o5[:, entries]), ACT.Copy)
+            nc.vector.tensor_tensor(diff[2][:, reads], pw[2][:].indirect(o4[:, entries]), from_pv[2][:, reads], ALU.subtract)
+        by_line = diff_all[:].rearrange("p (t h c i) -> p h c t i", t=PACK, h=2, i=4)
+        for h in range(2):
+            nc.scalar.activation(hid[h][:].rearrange("p (c i t) -> p c t i", i=4, t=PACK), by_line[:, h], ACT.Abs)
 
-        reuse = {(0, 0): "bank_a0", (0, 1): "bank_a1", (1, 0): "bank_p0", (1, 1): "bank_p1"}
         banks_p = {}
         for h in range(2):
             reads = slice(h * half, (h + 1) * half)
             for nt in range(N // P):
                 cols = slice(nt * P, (nt + 1) * P)
-                banks_p[h, nt] = ps.tile([P, half], F32, name="p_%d_%d" % (h, nt), tag=reuse[h, nt])
+                banks_p[h, nt] = ps.tile([P, half], F32, name="p_%d_%d" % (h, nt), tag="bank_a%d" % (2 * h + nt))
                 nc.tensor.matmul_mx(out=banks_p[h, nt][:], lhsT=ws_q[:, cols].bitcast(E2M1), lhsT_scale=ws_plane[:, cols],
                                     rhs=sx_q[:, reads].bitcast(E4M3), rhs_scale=sx_plane[:, reads], start=True, stop=False)
         p_sb = [tile("p_sb%d" % nt, O, F32) for nt in range(N // P)]
-        hid = [tile("hid%d" % h, PACK * half, BF16) for h in range(2)]
-        for h in range(2):
-            nc.vector.tensor_copy(hid[h][:].bitcast(I32).rearrange("p (o w) -> p o w", w=2),
-                                  pairs[h][:].bitcast(I32).rearrange("p (w o) -> p o w", w=2))
         for h in range(2):
             hid_q = tile("hid_q%d" % h, half, U32)
             hid_sc = tile("hid_sc%d" % h, half, U8)
@@ -222,10 +195,9 @@ def tile_list_twow_twoboards_skip_bestoftwo_kernel(
 
         first = [tile("first%d" % nt, E, F32) for nt in range(N // P)]
         second = [tile("second%d" % nt, E, F32) for nt in range(N // P)]
-        nc.scalar.activation(first[1][:], p_sb[1][:].indirect(o6[:]), ACT.Copy)
-        nc.scalar.activation(second[1][:], p_sb[1][:].indirect(o7[:]), ACT.Copy)
-        nc.vector.tensor_copy(first[0][:], p_sb[0][:].indirect(o6[:]))
-        nc.vector.tensor_copy(second[0][:], p_sb[0][:].indirect(o7[:]))
+        for nt in (1, 0):
+            nc.vector.tensor_copy(first[nt][:], p_sb[nt][:].indirect(o6[:]))
+            nc.scalar.activation(second[nt][:], p_sb[nt][:].indirect(o7[:]), ACT.Copy)
         for nt in (1, 0):
             best = tile("best%d" % nt, E, F32)
             nc.vector.tensor_tensor(best[:], first[nt][:], second[nt][:], ALU.max)

from contextlib import ExitStack

import concourse.mybir as mybir

K, T, J, R, C, O, N, L, E = 512, 1024, 256, 512, 512, 256, 256, 512, 128
FLOPS = 2 * (2 * K * R * J + R * N * O + L * N * O)

F32 = mybir.dt.float32
BF16 = mybir.dt.bfloat16
I32 = mybir.dt.int32
U32 = mybir.dt.uint32
U16 = mybir.dt.uint16
U8 = mybir.dt.uint8
E4M3 = mybir.dt.float8_e4m3fn_x4
E5M2 = mybir.dt.float8_e5m2_x4
E2M1 = mybir.dt.float4_e2m1fn_x4
ACT = mybir.ActivationFunctionType
ALU = mybir.AluOpType

P = 128
PACK = 4
QUADS = 4


def tile_list_twow_twoboards_skip_bestoftwo_kernel(
    tc, xt_words, xt_scales, w_words, w_scales, w2_words, w2_scales, wb_words, wb_scales,
    sx_words, sx_scales, ws_words, ws_scales, offs, offs2, offs3, offs4, offs5, offs6, offs7, out,
):
    nc = tc.nc
    with ExitStack() as ctx:
        lists = ctx.enter_context(tc.tile_pool(name="lists", bufs=1))
        sb = ctx.enter_context(tc.tile_pool(name="sb", bufs=1))
        ps = ctx.enter_context(tc.psum_pool(name="ps", bufs=1))

        stage = ctx.enter_context(tc.tile_pool(name="stage", bufs=1))
        board_bytes = 4 * C
        places = {"w_plane": 0, "xt_raw": board_bytes, "xt_plane": 3 * board_bytes, "w_raw": 3 * board_bytes + T,
                  "w2_plane": 4 * board_bytes, "w2_sc": 5 * board_bytes,
                  "pw2": 0, "pw3": board_bytes, "pv1": 2 * board_bytes, "pv0": 3 * board_bytes,
                  "pv3": 4 * board_bytes, "pv2": 5 * board_bytes,
                  "w2_q": 6 * board_bytes, "from_pw3": 6 * board_bytes}

        def tile(name, cols, dtype):
            if name in places:
                return stage.tile([P, cols], dtype, name=name, align_bytes=64, offset=places[name])
            return sb.tile([P, cols], dtype, name=name, align_bytes=64)

        def load_list(name, src):
            t = lists.tile([P, src.shape[1]], U16, name=name)
            nc.sync.dma_start(t[:], src)
            return t

        def load_words8(queue, name, src, cols):
            t = tile(name, cols, U32)
            queue.dma_start(t[:].bitcast(I32), src[0].rearrange("p n t -> p (n t)").bitcast(I32))
            return t

        def load_words4(queue, name, src, cols):
            t = tile(name, cols, U16)
            queue.dma_start(t[:].bitcast(I32), src[0].bitcast(I32))
            return t

        def zero_plane(name, cols):
            t = tile(name, cols, U8)
            nc.vector.memset(t[:].bitcast(I32), 0)
            return t

        def load_plane(queue, t, src, quads):
            for q in quads:
                queue.dma_start(t[32 * q : 32 * q + 4, :].bitcast(I32), src[0, 4 * q : 4 * q + 4, :].bitcast(I32))

        xt_plane = zero_plane("xt_plane", T)
        w_plane = zero_plane("w_plane", R)
        w2_plane = zero_plane("w2_plane", R)
        pw = [tile("pw%d" % t, C, F32) for t in range(PACK)]
        pv = [tile("pv%d" % t, C, F32) for t in range(PACK)]
        for board in (pw[0], pw[1]):
            nc.vector.memset(board[:], 0.0)
        ws_plane = tile("ws_plane", N, U8)
        sx_plane = tile("sx_plane", O, U8)
        wb_plane = tile("wb_plane", N, U8)

        w_rows = sb.tile([4, QUADS, R // 4], I32, name="w_rows", align_bytes=64)
        nc.sync.dma_start(w_rows[:], w_scales[0].bitcast(I32).rearrange("(q r) c -> r q c", q=QUADS))
        o1 = load_list("o1", offs)
        xt_raw = load_words8(nc.sync, "xt_raw", xt_words, T)
        w_raw = load_words4(nc.sync, "w_raw", w_words, R)
        load_plane(nc.sync, xt_plane, xt_scales, range(QUADS))
        w2_raw = load_words8(nc.sync, "w2_raw", w2_words, R)
        o2 = load_list("o2", offs2)
        load_plane(nc.sync, w2_plane, w2_scales, range(QUADS))
        o3 = load_list("o3", offs3)
        o4 = load_list("o4", offs4)
        o5 = load_list("o5", offs5)
        ws_q = load_words4(nc.sync, "ws_q", ws_words, N)
        sx_q = load_words8(nc.sync, "sx_q", sx_words, O)
        wb_q = load_words4(nc.sync, "wb_q", wb_words, N)
        load_plane(nc.sync, ws_plane, ws_scales, range(QUADS))
        load_plane(nc.sync, sx_plane, sx_scales, range(QUADS))
        load_plane(nc.sync, wb_plane, wb_scales, range(QUADS))
        o6 = load_list("o6", offs6)
        o7 = load_list("o7", offs7)

        for q in range(QUADS):
            nc.vector.tensor_copy(w_plane[32 * q : 32 * q + 4, :].bitcast(I32), w_rows[:, q, :])
        w_sc = tile("w_sc", R, U8)
        nc.vector.tensor_copy(w_sc[:].rearrange("p (t m) -> p t m", t=PACK), w_plane[:].rearrange("p (m t) -> p t m", t=PACK))
        nc.gpsimd.memset(pw[2][:], 0.0)
        w_q = tile("w_q", R, U16)
        nc.scalar.copy(w_q[:].rearrange("p (t m) -> p t m", t=PACK), w_raw[:].rearrange("p (m t) -> p t m", t=PACK))
        xg_q = tile("xg_q", J, U32)
        nc.vector.tensor_copy(xg_q[:], xt_raw[:].indirect(o1[:]))
        xg_plane = tile("xg_plane", J, U8)
        nc.vector.tensor_copy(xg_plane[:], xt_plane[:].indirect(o1[:]))

        w2_q = tile("w2_q", R, U32)
        nc.vector.tensor_copy(w2_q[:].rearrange("p (t m) -> p m t", t=PACK), w2_raw[:].rearrange("p (m t) -> p m t", t=PACK))

        def first_stage(dst, words, scales, fmt, t):
            cols = slice(t * P, (t + 1) * P)
            nc.tensor.matmul_mx(out=dst, lhsT=words[:, cols].bitcast(fmt), lhsT_scale=scales[:, cols],
                                rhs=xg_q[:].bitcast(E5M2), rhs_scale=xg_plane[:], start=True, stop=True)

        a_ps = [ps.tile([P, J], F32, name="a_ps%d" % t, tag="bank_a%d" % t) for t in range(PACK)]
        b_ps = [ps.tile([P, 2 * J], F32, name="b_ps%d" % u) for u in range(2)]
        for t in range(PACK):
            first_stage(a_ps[t][:], w_q, w_sc, E2M1, t)
        w2_sc = tile("w2_sc", R, U8)
        nc.gpsimd.tensor_copy(w2_sc[:].rearrange("p (t m) -> p t m", t=PACK), w2_plane[:].rearrange("p (m t) -> p t m", t=PACK))
        for t in range(PACK):
            first_stage(b_ps[t // 2][:, (t % 2) * J : (t % 2 + 1) * J], w2_q, w2_sc, E4M3, t)
        for board in (pw[3], pv[1], pv[0], pv[3], pv[2]):
            nc.gpsimd.memset(board[:], 0.0)

        a_sb = [tile("a%d" % t, J, F32) for t in range(PACK)]
        b_sb = [tile("b%d" % u, 2 * J, F32) for u in range(2)]
        from_pw = {t: tile("from_pw%d" % t, O, F32) for t in (0, 1, 3)}
        from_pv = {t: tile("from_pv%d" % t, O, F32) for t in (0, 1, 2)}
        diff_all = tile("diff", PACK * O, F32)
        diff = [diff_all[:, t * O : (t + 1) * O] for t in range(PACK)]

        for t in (0, 2):
            nc.vector.tensor_copy(a_sb[t][:], a_ps[t][:])
            nc.scalar.copy(a_sb[t + 1][:], a_ps[t + 1][:])
        for t in (0, 2):
            nc.vector.tensor_copy(pw[t][:].indirect(o2[:]), a_sb[t][:])
            nc.scalar.activation(pw[t + 1][:].indirect(o2[:]), a_sb[t + 1][:], ACT.Copy)
        nc.scalar.activation(from_pw[1][:], pw[1][:].indirect(o4[:]), ACT.Copy)
        nc.vector.tensor_copy(from_pw[0][:], pw[0][:].indirect(o4[:]))
        nc.vector.tensor_copy(b_sb[0][:], b_ps[0][:])
        nc.scalar.activation(pv[0][:].indirect(o3[:]), b_sb[0][:, 0:J], ACT.Copy)
        nc.vector.tensor_copy(pv[1][:].indirect(o3[:]), b_sb[0][:, J : 2 * J])
        nc.scalar.copy(b_sb[1][:], b_ps[1][:])
        nc.scalar.activation(from_pw[3][:], pw[3][:].indirect(o4[:]), ACT.Copy)
        nc.scalar.activation(from_pv[0][:], pv[0][:].indirect(o5[:]), ACT.Copy)
        nc.vector.tensor_copy(from_pv[1][:], pv[1][:].indirect(o5[:]))
        nc.scalar.activation(pv[2][:].indirect(o3[:]), b_sb[1][:, 0:J], ACT.Copy)
        nc.vector.tensor_copy(pv[3][:].indirect(o3[:]), b_sb[1][:, J : 2 * J])
        for t in (1, 0):
            nc.gpsimd.tensor_tensor(diff[t], from_pw[t][:], from_pv[t][:], ALU.subtract)
        nc.vector.tensor_tensor(diff[3], pv[3][:].indirect(o5[:]), from_pw[3][:], ALU.subtract)
        half = O // 2
        hid = [tile("hid%d" % h, PACK * half, BF16) for h in range(2)]
        for h in range(2):
            reads = slice(h * half, (h + 1) * half)
            entries = slice(h * half // 16, (h + 1) * half // 16)
            nc.scalar.activation(from_pv[2][:, reads], pv[2][:].indirect(o5[:, entries]), ACT.Copy)
            nc.vector.tensor_tensor(diff[2][:, reads], pw[2][:].indirect(o4[:, entries]), from_pv[2][:, reads], ALU.subtract)
        by_line = diff_all[:].rearrange("p (t h c i) -> p h c t i", t=PACK, h=2, i=4)
        for h in range(2):
            nc.scalar.activation(hid[h][:].rearrange("p (c i t) -> p c t i", i=4, t=PACK), by_line[:, h], ACT.Abs)

        banks_p = {}
        for h in range(2):
            reads = slice(h * half, (h + 1) * half)
            for nt in range(N // P):
                cols = slice(nt * P, (nt + 1) * P)
                banks_p[h, nt] = ps.tile([P, half], F32, name="p_%d_%d" % (h, nt), tag="bank_a%d" % (2 * h + nt))
                nc.tensor.matmul_mx(out=banks_p[h, nt][:], lhsT=ws_q[:, cols].bitcast(E2M1), lhsT_scale=ws_plane[:, cols],
                                    rhs=sx_q[:, reads].bitcast(E4M3), rhs_scale=sx_plane[:, reads], start=True, stop=False)
        p_sb = [tile("p_sb%d" % nt, O, F32) for nt in range(N // P)]
        for h in range(2):
            hid_q = tile("hid_q%d" % h, half, U32)
            hid_sc = tile("hid_sc%d" % h, half, U8)
            nc.vector.quantize_mx(out=hid_q[:].bitcast(E4M3), scales=hid_sc[:], in_=hid[h][:])
            for nt in (1, 0):
                cols = slice(nt * P, (nt + 1) * P)
                nc.tensor.matmul_mx(out=banks_p[h, nt][:], lhsT=wb_q[:, cols].bitcast(E2M1),
                                    lhsT_scale=wb_plane[:, cols], rhs=hid_q[:].bitcast(E4M3), rhs_scale=hid_sc[:],
                                    start=False, stop=True)
                if h == 1 and nt == 0:
                    nc.vector.tensor_copy(p_sb[nt][:, half:O], banks_p[h, nt][:])
                else:
                    nc.scalar.copy(p_sb[nt][:, h * half : (h + 1) * half], banks_p[h, nt][:])

        first = [tile("first%d" % nt, E, F32) for nt in range(N // P)]
        second = [tile("second%d" % nt, E, F32) for nt in range(N // P)]
        for nt in (1, 0):
            nc.vector.tensor_copy(first[nt][:], p_sb[nt][:].indirect(o6[:]))
            nc.scalar.activation(second[nt][:], p_sb[nt][:].indirect(o7[:]), ACT.Copy)
        for nt in (1, 0):
            best = tile("best%d" % nt, E, F32)
            nc.vector.tensor_tensor(best[:], first[nt][:], second[nt][:], ALU.max)
            nc.sync.dma_start(out[nt * P : (nt + 1) * P, :], best[:])
